import numpy as np
import ml_dtypes


def mxq(x, axis, fmt="e4m3"):
    dtype, down = {"e4m3": (ml_dtypes.float8_e4m3fn, 7), "e5m2": (ml_dtypes.float8_e5m2, 14)}[fmt]
    v = np.moveaxis(np.asarray(x, np.float32).astype(ml_dtypes.bfloat16).astype(np.float64), axis, -1)
    blocks = v.reshape(v.shape[:-1] + (-1, 32))
    amax = np.abs(blocks).max(-1, keepdims=True)
    byte = np.maximum(np.where(amax > 0, np.frexp(amax)[1] - 1 + 127, 0) - down, 1)
    scale = np.exp2(byte - 127.0)
    codes = (blocks / scale).astype(np.float32).astype(dtype).astype(np.float64)
    return np.moveaxis((codes * scale).reshape(v.shape), -1, axis)


WIDE = False


def mx_kscale(k):
    if not WIDE:
        return np.ones(k)
    levels = np.array([10, -10, 5, -5, 0])
    if k % 512:
        return np.exp2(np.random.permutation(np.resize(levels, k // 32))).repeat(32)
    a = np.empty((k // 512, 16))
    for p in range(k // 512):
        a[p, :8] = np.random.permutation(np.resize(levels, 8))
        for g in range(8):
            far = levels[np.abs(levels - a[p, g]) >= 10]
            a[p, g + 8] = far[np.random.randint(len(far))]
    return np.exp2(a.ravel()).repeat(32)


def f64(x):
    return np.asarray(x).astype(np.float64)


def striped(idx):
    return np.tile(idx.reshape(-1, 16).T, (8, 1)).astype(np.uint16)


def unstriped(offs):
    return offs[:16].T.reshape(-1).astype(np.int64)


def pack_weight(w):
    k, n = w.shape
    w = f64(np.asarray(w, np.float32).astype(ml_dtypes.bfloat16)).reshape(k // 32, 32, n)
    amax = np.abs(w).max(1)
    byte = np.clip(np.where(amax > 0, np.frexp(amax)[1] - 1 + 127 - 7, 1), 1, 254)
    scaled = (w * np.exp2(127.0 - byte)[:, None, :]).reshape(k, n).astype(np.float32)
    words = np.ascontiguousarray(scaled.reshape(k // 512, 128, 4, n).transpose(0, 1, 3, 2)).astype(ml_dtypes.float8_e4m3fn).view(np.uint8)
    return words, np.ascontiguousarray(byte.astype(np.uint8).reshape(k // 512, 16, n))


def unpack_weight(words, scales):
    g, p, n, _ = words.shape
    vals = np.ascontiguousarray(words).view(ml_dtypes.float8_e4m3fn).astype(np.float64) * np.repeat(np.exp2(scales.astype(np.float64) - 127.0), 8, axis=1)[..., None]
    return vals.transpose(0, 1, 3, 2).reshape(g * 512, n)


K, T, S, N = 512, 2048, 1024, 128
P = 2 ** 7


def setup_inputs():
    n = np.random.standard_normal
    s = mx_kscale(K)[:, None]
    packed_w1 = pack_weight(n((K, N)) / np.sqrt(K) / s)
    return {
        "xT": (n((K, T)) * s).astype(np.float32),
        "tscale": np.tile(np.random.uniform(0.25, 2.0, T), (P, 1)).astype(np.float32),
        "cscale": np.random.uniform(0.5, 1.5, (N, 1)).astype(np.float32),
        "w1_words": packed_w1[0],
        "w1_scales": packed_w1[1],
        "offs": striped(np.random.permutation(T)[:S]),
    }


def reference(xT, tscale, cscale, w1_words, w1_scales, offs):
    xq = mxq(f64(xT)[:, unstriped(offs)], 0, "e4m3")
    y = unpack_weight(w1_words, w1_scales).T @ xq
    tg = f64(tscale)[:1][:, unstriped(offs)]
    return (f64(cscale) * y) * tg

@@ -1,0 +1,121 @@
+from contextlib import ExitStack
+
+import concourse.mybir as mybir
+from concourse.masks import make_identity
+
+K, T, S, N = 512, 2048, 1024, 128
+FLOPS = 2 * K * N * S
+BYTES = 4 * K * T + 4 * T + 4 * N + K * N + 16 * N + 2 * 128 * (S // 16) + 4 * N * S
+
+F32 = mybir.dt.float32
+BF16 = mybir.dt.bfloat16
+U32 = mybir.dt.uint32
+I32 = mybir.dt.int32
+U16 = mybir.dt.uint16
+U8 = mybir.dt.uint8
+FP8X4 = mybir.dt.float8_e4m3fn_x4
+MULT = mybir.AluOpType.mult
+
+P = 128
+CHUNK = 256
+CHUNKS = S // CHUNK
+LOADS = [(0, 0, 1024, 1024), (0, 1024, 1024, 768), (1, 1024, 1024, 1024), (1, 0, 512, 0), (1, 512, 256, 256), (1, 768, 256, 0)]
+PAIR_START = [0, 1024]
+SCALE_START = 1792
+
+
+def tile_picked_tokscale_none_l_kernel(tc, xT, tscale, cscale, w1_words, w1_scales, offs, out):
+    nc = tc.nc
+    with ExitStack() as ctx:
+        keep = ctx.enter_context(tc.tile_pool(name="keep", bufs=1))
+        psum = ctx.enter_context(tc.psum_pool(name="psum", bufs=1))
+
+        offsets = keep.tile([P, S // 16], U16, name="offsets")
+        x_rows = xT.rearrange("(p u e) t -> u p e t", u=2, e=2)
+        raw = [keep.tile([P, 2, width], F32, name=f"raw{i}") for i, (u, t0, width, cut) in enumerate(LOADS)]
+
+        arena = keep.tile([P, SCALE_START + T], U32, name="arena")
+        pairs = [arena[:, start : start + T] for start in PAIR_START]
+        t_window = arena[:, SCALE_START : SCALE_START + T].bitcast(F32)
+        t_row = keep.tile([P, 16], F32, name="t_row")
+        nc.sync.dma_start(out=t_row[:], in_=tscale[0].rearrange("(p j) -> p j", j=16))
+        for i, (u, t0, width, cut) in enumerate(LOADS):
+            nc.sync.dma_start(out=raw[i][:], in_=x_rows[u][:, :, t0 : t0 + width])
+            if i == 0:
+                nc.sync.dma_start(offsets[:], offs)
+
+        w_codes = keep.tile([P, N], U32, name="w_codes", align_bytes=64)
+        w_scales = keep.tile([P, N], U8, name="w_scales", align_bytes=64)
+        c_col = keep.tile([P, 1], F32, name="c_col")
+        nc.vector.memset(w_scales[:].bitcast(I32), 0)
+        nc.sync.dma_start(out=w_codes[:].bitcast(I32), in_=w1_words[0].rearrange("p n r -> p (n r)").bitcast(I32))
+        for q in range(4):
+            nc.sync.dma_start(out=w_scales[32 * q : 32 * q + 4, :].bitcast(I32), in_=w1_scales[0][4 * q : 4 * q + 4, :].bitcast(I32))
+        nc.sync.dma_start(out=c_col[:], in_=cscale)
+
+        identity = keep.tile([P, P], F32, name="identity")
+        make_identity(nc, identity[:])
+        t_view = t_window.rearrange("f (p a i) -> f a p i", a=4, i=4)
+        for a in range(4):
+            bank = psum.tile([P, 4, P], F32, name=f"t_bank{a}")
+            for i in range(4):
+                column = t_row[:, 4 * a + i : 4 * a + i + 1]
+                nc.tensor.transpose(bank[:, i, :], column.to_broadcast([P, P]), identity[:])
+            nc.vector.tensor_copy(out=t_view[:, a], in_=bank[:].rearrange("f i p -> f p i"))
+        t_picked = keep.tile([P, S], F32, name="t_picked")
+        nc.vector.tensor_copy(out=t_picked[:], in_=t_window.indirect(offsets[:]))
+
+        picked = [keep.tile([P, 2, CHUNK], U32, name=f"picked{c}") for c in range(CHUNKS)]
+
+        def cast(i):
+            u, t0, width, cut = LOADS[i]
+            dst = pairs[u].bitcast(BF16).rearrange("p (t e) -> p t e", e=2)
+            src = raw[i][:].rearrange("p e t -> p t e")
+            if cut > 0:
+                nc.scalar.copy(out=dst[:, t0 : t0 + cut, :], in_=src[:, 0:cut, :])
+            if cut < width:
+                nc.vector.tensor_copy(out=dst[:, t0 + cut : t0 + width, :], in_=src[:, cut:width, :])
+
+        def gather(u, c):
+            entries = offsets[:, c * (CHUNK // 16) : (c + 1) * (CHUNK // 16)]
+            nc.vector.tensor_copy(out=picked[c][:, u, :], in_=pairs[u].indirect(entries))
+
+        for i, load in enumerate(LOADS):
+            if load[0] == 0:
+                cast(i)
+        for c in range(CHUNKS):
+            gather(0, c)
+        for i, load in enumerate(LOADS):
+            if load[0] == 1:
+                cast(i)
+
+        woven = [keep.tile([P, CHUNK, 2], U32, name=f"woven{c}", align_bytes=64) for c in range(CHUNKS)]
+        x_codes = [keep.tile([P, CHUNK], U32, name=f"x_codes{c}", align_bytes=64) for c in range(CHUNKS)]
+        x_scales = [keep.tile([P, CHUNK], U8, name=f"x_scales{c}", align_bytes=64) for c in range(CHUNKS)]
+        acc = [psum.tile([P, CHUNK], F32, name=f"acc{c}") for c in range(CHUNKS)]
+        result = [keep.tile([P, CHUNK], F32, name=f"result{c}") for c in range(CHUNKS)]
+
+        for c in range(CHUNKS):
+            gather(1, c)
+            nc.scalar.copy(out=woven[c][:], in_=picked[c][:].rearrange("p u n -> p n u"))
+        for c in range(CHUNKS):
+            nc.vector.quantize_mx(
+                out=x_codes[c][:].bitcast(FP8X4),
+                scales=x_scales[c][:],
+                in_=woven[c][:].rearrange("p n u -> p (n u)").bitcast(BF16),
+            )
+            nc.tensor.matmul_mx(
+                out=acc[c][:],
+                lhsT=w_codes[:].bitcast(FP8X4),
+                lhsT_scale=w_scales[:],
+                rhs=x_codes[c][:].bitcast(FP8X4),
+                rhs_scale=x_scales[c][:],
+                start=True,
+                stop=True,
+            )
+        for c in range(CHUNKS):
+            cols = slice(c * CHUNK, (c + 1) * CHUNK)
+            nc.vector.scalar_tensor_tensor(
+                out=result[c][:], in0=acc[c][:], scalar=c_col[:, 0:1], in1=t_picked[:, cols], op0=MULT, op1=MULT
+            )
+            nc.sync.dma_start(out=out[:, cols], in_=result[c][:])

@@ -19,9 +19,8 @@ MULT = mybir.AluOpType.mult
 P = 128
 CHUNK = 256
 CHUNKS = S // CHUNK
-LOADS = [(0, 0, 1024, 1024), (0, 1024, 1024, 768), (1, 1024, 1024, 1024), (1, 0, 512, 0), (1, 512, 256, 256), (1, 768, 256, 0)]
+LOADS = [(0, 0, 1024, 1024), (0, 1024, 512, 0), (0, 1536, 512, 176), (1, 1024, 1024, 640), (1, 0, 512, 0), (1, 512, 512, 176)]
 PAIR_START = [0, 1024]
-SCALE_START = 1792
 
 
 def tile_picked_tokscale_none_l_kernel(tc, xT, tscale, cscale, w1_words, w1_scales, offs, out):
@@ -34,15 +33,15 @@ def tile_picked_tokscale_none_l_kernel(tc, xT, tscale, cscale, w1_words, w1_scal
         x_rows = xT.rearrange("(p u e) t -> u p e t", u=2, e=2)
         raw = [keep.tile([P, 2, width], F32, name=f"raw{i}") for i, (u, t0, width, cut) in enumerate(LOADS)]
 
-        arena = keep.tile([P, SCALE_START + T], U32, name="arena")
+        arena = keep.tile([P, PAIR_START[1] + T], U32, name="arena")
         pairs = [arena[:, start : start + T] for start in PAIR_START]
-        t_window = arena[:, SCALE_START : SCALE_START + T].bitcast(F32)
-        t_row = keep.tile([P, 16], F32, name="t_row")
-        nc.sync.dma_start(out=t_row[:], in_=tscale[0].rearrange("(p j) -> p j", j=16))
+        t_row = arena[:, T : T + S].bitcast(F32)
+        t_window = keep.tile([P, T], F32, name="t_window")
+        nc.vector.memset(t_window[0 : P - 1, :], 0.0)
+        nc.sync.dma_start(out=t_window[P - 1 : P, :], in_=tscale[0:1, :])
+        nc.sync.dma_start(offsets[:], offs)
         for i, (u, t0, width, cut) in enumerate(LOADS):
             nc.sync.dma_start(out=raw[i][:], in_=x_rows[u][:, :, t0 : t0 + width])
-            if i == 0:
-                nc.sync.dma_start(offsets[:], offs)
 
         w_codes = keep.tile([P, N], U32, name="w_codes", align_bytes=64)
         w_scales = keep.tile([P, N], U8, name="w_scales", align_bytes=64)
@@ -55,15 +54,23 @@ def tile_picked_tokscale_none_l_kernel(tc, xT, tscale, cscale, w1_words, w1_scal
 
         identity = keep.tile([P, P], F32, name="identity")
         make_identity(nc, identity[:])
-        t_view = t_window.rearrange("f (p a i) -> f a p i", a=4, i=4)
-        for a in range(4):
-            bank = psum.tile([P, 4, P], F32, name=f"t_bank{a}")
-            for i in range(4):
-                column = t_row[:, 4 * a + i : 4 * a + i + 1]
-                nc.tensor.transpose(bank[:, i, :], column.to_broadcast([P, P]), identity[:])
-            nc.vector.tensor_copy(out=t_view[:, a], in_=bank[:].rearrange("f i p -> f p i"))
+        nc.vector.tensor_copy(out=t_row, in_=t_window[:].indirect(offsets[:]))
         t_picked = keep.tile([P, S], F32, name="t_picked")
-        nc.vector.tensor_copy(out=t_picked[:], in_=t_window.indirect(offsets[:]))
+        woven = [keep.tile([P, CHUNK, 2], U32, name=f"woven{c}", align_bytes=64) for c in range(CHUNKS)]
+        t_col = t_row[:, 0:8]
+        wide = [psum.tile([P, 4, P], F32, name=f"wide{h}") for h in range(2)]
+
+        def turn(h):
+            turned = psum.tile([P, 4, P], F32, name=f"turned{h}")
+            for i in range(4):
+                nc.tensor.transpose(turned[:, i, :], t_row[:, (4 * h + i) * P : (4 * h + i + 1) * P], identity[:])
+            nc.scalar.copy(out=t_col[:, 4 * h : 4 * h + 4], in_=turned[:, :, P - 1])
+
+        def spread(h):
+            for i in range(4):
+                column = t_col[:, 4 * h + i : 4 * h + i + 1]
+                nc.tensor.transpose(wide[h][:, i, :], column.to_broadcast([P, P]), identity[:])
+            nc.scalar.copy(out=t_picked[:, 4 * h * P : 4 * (h + 1) * P], in_=wide[h][:].rearrange("f i p -> f (i p)"))
 
         picked = [keep.tile([P, 2, CHUNK], U32, name=f"picked{c}") for c in range(CHUNKS)]
 
@@ -83,13 +90,16 @@ def tile_picked_tokscale_none_l_kernel(tc, xT, tscale, cscale, w1_words, w1_scal
         for i, load in enumerate(LOADS):
             if load[0] == 0:
                 cast(i)
+        for h in range(2):
+            turn(h)
+        for h in range(2):
+            spread(h)
         for c in range(CHUNKS):
             gather(0, c)
         for i, load in enumerate(LOADS):
             if load[0] == 1:
                 cast(i)
 
-        woven = [keep.tile([P, CHUNK, 2], U32, name=f"woven{c}", align_bytes=64) for c in range(CHUNKS)]
         x_codes = [keep.tile([P, CHUNK], U32, name=f"x_codes{c}", align_bytes=64) for c in range(CHUNKS)]
         x_scales = [keep.tile([P, CHUNK], U8, name=f"x_scales{c}", align_bytes=64) for c in range(CHUNKS)]
         acc = [psum.tile([P, CHUNK], F32, name=f"acc{c}") for c in range(CHUNKS)]

@@ -19,7 +19,7 @@ MULT = mybir.AluOpType.mult
 P = 128
 CHUNK = 256
 CHUNKS = S // CHUNK
-LOADS = [(0, 0, 1024, 1024), (0, 1024, 512, 0), (0, 1536, 512, 176), (1, 1024, 1024, 640), (1, 0, 512, 0), (1, 512, 512, 176)]
+LOADS = [(0, 0, 1024, 1024), (0, 1024, 512, 0), (0, 1536, 512, 176), (1, 1024, 1024, 576), (1, 0, 512, 0), (1, 512, 512, 176)]
 PAIR_START = [0, 1024]
 
 
@@ -57,7 +57,7 @@ def tile_picked_tokscale_none_l_kernel(tc, xT, tscale, cscale, w1_words, w1_scal
         nc.vector.tensor_copy(out=t_row, in_=t_window[:].indirect(offsets[:]))
         t_picked = keep.tile([P, S], F32, name="t_picked")
         woven = [keep.tile([P, CHUNK, 2], U32, name=f"woven{c}", align_bytes=64) for c in range(CHUNKS)]
-        t_col = t_row[:, 0:8]
+        t_col = woven[0][:].rearrange("p n u -> p (n u)")[:, 0:8].bitcast(F32)
         wide = [psum.tile([P, 4, P], F32, name=f"wide{h}") for h in range(2)]
 
         def turn(h):
@@ -92,13 +92,13 @@ def tile_picked_tokscale_none_l_kernel(tc, xT, tscale, cscale, w1_words, w1_scal
                 cast(i)
         for h in range(2):
             turn(h)
-        for h in range(2):
-            spread(h)
         for c in range(CHUNKS):
             gather(0, c)
         for i, load in enumerate(LOADS):
             if load[0] == 1:
                 cast(i)
+        for h in range(2):
+            spread(h)
 
         x_codes = [keep.tile([P, CHUNK], U32, name=f"x_codes{c}", align_bytes=64) for c in range(CHUNKS)]
         x_scales = [keep.tile([P, CHUNK], U8, name=f"x_scales{c}", align_bytes=64) for c in range(CHUNKS)]

@@ -19,7 +19,7 @@ MULT = mybir.AluOpType.mult
 P = 128
 CHUNK = 256
 CHUNKS = S // CHUNK
-LOADS = [(0, 0, 1024, 1024), (0, 1024, 512, 0), (0, 1536, 512, 176), (1, 1024, 1024, 576), (1, 0, 512, 0), (1, 512, 512, 176)]
+LOADS = [(0, 0, 1024, 1024), (0, 1024, 512, 0), (0, 1536, 512, 176), (1, 1024, 1024, 1024), (1, 0, 512, 0), (1, 512, 512, 176)]
 PAIR_START = [0, 1024]
 
 
@@ -55,7 +55,6 @@ def tile_picked_tokscale_none_l_kernel(tc, xT, tscale, cscale, w1_words, w1_scal
         identity = keep.tile([P, P], F32, name="identity")
         make_identity(nc, identity[:])
         nc.vector.tensor_copy(out=t_row, in_=t_window[:].indirect(offsets[:]))
-        t_picked = keep.tile([P, S], F32, name="t_picked")
         woven = [keep.tile([P, CHUNK, 2], U32, name=f"woven{c}", align_bytes=64) for c in range(CHUNKS)]
         t_col = woven[0][:].rearrange("p n u -> p (n u)")[:, 0:8].bitcast(F32)
         wide = [psum.tile([P, 4, P], F32, name=f"wide{h}") for h in range(2)]
@@ -70,9 +69,12 @@ def tile_picked_tokscale_none_l_kernel(tc, xT, tscale, cscale, w1_words, w1_scal
             for i in range(4):
                 column = t_col[:, 4 * h + i : 4 * h + i + 1]
                 nc.tensor.transpose(wide[h][:, i, :], column.to_broadcast([P, P]), identity[:])
-            nc.scalar.copy(out=t_picked[:, 4 * h * P : 4 * (h + 1) * P], in_=wide[h][:].rearrange("f i p -> f (i p)"))
+
+        def fetch(h):
+            nc.scalar.copy(out=t_picked[h], in_=wide[h][:].rearrange("f i p -> f (i p)"))
 
         picked = [keep.tile([P, 2, CHUNK], U32, name=f"picked{c}") for c in range(CHUNKS)]
+        t_picked = [raw[-1][:, 0, :], picked[-1][:].rearrange("p u n -> p (u n)").bitcast(F32)]
 
         def cast(i):
             u, t0, width, cut = LOADS[i]
@@ -99,6 +101,7 @@ def tile_picked_tokscale_none_l_kernel(tc, xT, tscale, cscale, w1_words, w1_scal
                 cast(i)
         for h in range(2):
             spread(h)
+        fetch(0)
 
         x_codes = [keep.tile([P, CHUNK], U32, name=f"x_codes{c}", align_bytes=64) for c in range(CHUNKS)]
         x_scales = [keep.tile([P, CHUNK], U8, name=f"x_scales{c}", align_bytes=64) for c in range(CHUNKS)]
@@ -108,6 +111,7 @@ def tile_picked_tokscale_none_l_kernel(tc, xT, tscale, cscale, w1_words, w1_scal
         for c in range(CHUNKS):
             gather(1, c)
             nc.scalar.copy(out=woven[c][:], in_=picked[c][:].rearrange("p u n -> p n u"))
+        fetch(1)
         for c in range(CHUNKS):
             nc.vector.quantize_mx(
                 out=x_codes[c][:].bitcast(FP8X4),
@@ -125,7 +129,8 @@ def tile_picked_tokscale_none_l_kernel(tc, xT, tscale, cscale, w1_words, w1_scal
             )
         for c in range(CHUNKS):
             cols = slice(c * CHUNK, (c + 1) * CHUNK)
+            factor = t_picked[c // 2][:, (c % 2) * CHUNK : (c % 2 + 1) * CHUNK]
             nc.vector.scalar_tensor_tensor(
-                out=result[c][:], in0=acc[c][:], scalar=c_col[:, 0:1], in1=t_picked[:, cols], op0=MULT, op1=MULT
+                out=result[c][:], in0=acc[c][:], scalar=c_col[:, 0:1], in1=factor, op0=MULT, op1=MULT
             )
             nc.sync.dma_start(out=out[:, cols], in_=result[c][:])

@@ -15,12 +15,12 @@ U16 = mybir.dt.uint16
 U8 = mybir.dt.uint8
 FP8X4 = mybir.dt.float8_e4m3fn_x4
 MULT = mybir.AluOpType.mult
+COPY = mybir.ActivationFunctionType.Copy
 
 P = 128
 CHUNK = 256
 CHUNKS = S // CHUNK
-LOADS = [(0, 0, 1024, 1024), (0, 1024, 512, 0), (0, 1536, 512, 176), (1, 1024, 1024, 1024), (1, 0, 512, 0), (1, 512, 512, 176)]
-PAIR_START = [0, 1024]
+VECTOR_SHARE = [512, 256, 512]
 
 
 def tile_picked_tokscale_none_l_kernel(tc, xT, tscale, cscale, w1_words, w1_scales, offs, out):
@@ -30,18 +30,14 @@ def tile_picked_tokscale_none_l_kernel(tc, xT, tscale, cscale, w1_words, w1_scal
         psum = ctx.enter_context(tc.psum_pool(name="psum", bufs=1))
 
         offsets = keep.tile([P, S // 16], U16, name="offsets")
-        x_rows = xT.rearrange("(p u e) t -> u p e t", u=2, e=2)
-        raw = [keep.tile([P, 2, width], F32, name=f"raw{i}") for i, (u, t0, width, cut) in enumerate(LOADS)]
-
-        arena = keep.tile([P, PAIR_START[1] + T], U32, name="arena")
-        pairs = [arena[:, start : start + T] for start in PAIR_START]
-        t_row = arena[:, T : T + S].bitcast(F32)
+        x_rows = xT.rearrange("(p t) c -> t p c", t=4)
+        planes = [keep.tile([P, T], F32, name=f"plane{t}") for t in range(4)]
         t_window = keep.tile([P, T], F32, name="t_window")
         nc.vector.memset(t_window[0 : P - 1, :], 0.0)
         nc.sync.dma_start(out=t_window[P - 1 : P, :], in_=tscale[0:1, :])
         nc.sync.dma_start(offsets[:], offs)
-        for i, (u, t0, width, cut) in enumerate(LOADS):
-            nc.sync.dma_start(out=raw[i][:], in_=x_rows[u][:, :, t0 : t0 + width])
+        for t in range(4):
+            nc.sync.dma_start(out=planes[t][:], in_=x_rows[t])
 
         w_codes = keep.tile([P, N], U32, name="w_codes", align_bytes=64)
         w_scales = keep.tile([P, N], U8, name="w_scales", align_bytes=64)
@@ -52,71 +48,64 @@ def tile_picked_tokscale_none_l_kernel(tc, xT, tscale, cscale, w1_words, w1_scal
             nc.sync.dma_start(out=w_scales[32 * q : 32 * q + 4, :].bitcast(I32), in_=w1_scales[0][4 * q : 4 * q + 4, :].bitcast(I32))
         nc.sync.dma_start(out=c_col[:], in_=cscale)
 
+        def entries(lo, hi):
+            return offsets[:, lo // 16 : hi // 16]
+
+        def gather(on_vector, dst, window, lo, hi):
+            if on_vector:
+                nc.vector.tensor_copy(out=dst, in_=window[:].indirect(entries(lo, hi)))
+            else:
+                nc.scalar.activation(dst, window[:].indirect(entries(lo, hi)), COPY)
+
         identity = keep.tile([P, P], F32, name="identity")
         make_identity(nc, identity[:])
-        nc.vector.tensor_copy(out=t_row, in_=t_window[:].indirect(offsets[:]))
-        woven = [keep.tile([P, CHUNK, 2], U32, name=f"woven{c}", align_bytes=64) for c in range(CHUNKS)]
-        t_col = woven[0][:].rearrange("p n u -> p (n u)")[:, 0:8].bitcast(F32)
-        wide = [psum.tile([P, 4, P], F32, name=f"wide{h}") for h in range(2)]
-
-        def turn(h):
+        t_row = [keep.tile([P, 512], F32, name=f"t_row{h}") for h in range(2)]
+        t_col = [keep.tile([P, 4], F32, name=f"t_col{h}") for h in range(2)]
+        t_picked = [keep.tile([P, 512], F32, name=f"t_picked{h}") for h in range(2)]
+        for h in range(2):
+            gather(h == 0, t_row[h][:], t_window, 512 * h, 512 * (h + 1))
+        for h in range(2):
             turned = psum.tile([P, 4, P], F32, name=f"turned{h}")
             for i in range(4):
-                nc.tensor.transpose(turned[:, i, :], t_row[:, (4 * h + i) * P : (4 * h + i + 1) * P], identity[:])
-            nc.scalar.copy(out=t_col[:, 4 * h : 4 * h + 4], in_=turned[:, :, P - 1])
-
-        def spread(h):
+                nc.tensor.transpose(turned[:, i, :], t_row[h][:, i * P : (i + 1) * P], identity[:])
+            nc.scalar.copy(out=t_col[h][:], in_=turned[:, :, P - 1])
+        for h in range(2):
+            wide = psum.tile([P, 4, P], F32, name=f"wide{h}")
             for i in range(4):
-                column = t_col[:, 4 * h + i : 4 * h + i + 1]
-                nc.tensor.transpose(wide[h][:, i, :], column.to_broadcast([P, P]), identity[:])
+                nc.tensor.transpose(wide[:, i, :], t_col[h][:, i : i + 1].to_broadcast([P, P]), identity[:])
+            if h == 0:
+                nc.vector.tensor_copy(out=t_picked[h][:], in_=wide[:].rearrange("f i p -> f (i p)"))
+            else:
+                nc.scalar.copy(out=t_picked[h][:], in_=wide[:].rearrange("f i p -> f (i p)"))
 
-        def fetch(h):
-            nc.scalar.copy(out=t_picked[h], in_=wide[h][:].rearrange("f i p -> f (i p)"))
+        picked = [keep.tile([P, 4, CHUNK], BF16, name=f"picked{c}") for c in range(CHUNKS)]
+        woven = [keep.tile([P, CHUNK, 4], BF16, name=f"woven{c}", align_bytes=64) for c in range(CHUNKS)]
 
-        picked = [keep.tile([P, 2, CHUNK], U32, name=f"picked{c}") for c in range(CHUNKS)]
-        t_picked = [raw[-1][:, 0, :], picked[-1][:].rearrange("p u n -> p (u n)").bitcast(F32)]
+        def merge(on_vector, c, lo, hi):
+            src = picked[c][:, lo:hi, :].rearrange("p t n -> p n t")
+            if on_vector:
+                nc.vector.tensor_copy(out=woven[c][:, :, lo:hi], in_=src)
+            else:
+                nc.scalar.copy(out=woven[c][:, :, lo:hi], in_=src)
 
-        def cast(i):
-            u, t0, width, cut = LOADS[i]
-            dst = pairs[u].bitcast(BF16).rearrange("p (t e) -> p t e", e=2)
-            src = raw[i][:].rearrange("p e t -> p t e")
-            if cut > 0:
-                nc.scalar.copy(out=dst[:, t0 : t0 + cut, :], in_=src[:, 0:cut, :])
-            if cut < width:
-                nc.vector.tensor_copy(out=dst[:, t0 + cut : t0 + width, :], in_=src[:, cut:width, :])
-
-        def gather(u, c):
-            entries = offsets[:, c * (CHUNK // 16) : (c + 1) * (CHUNK // 16)]
-            nc.vector.tensor_copy(out=picked[c][:, u, :], in_=pairs[u].indirect(entries))
-
-        for i, load in enumerate(LOADS):
-            if load[0] == 0:
-                cast(i)
-        for h in range(2):
-            turn(h)
-        for c in range(CHUNKS):
-            gather(0, c)
-        for i, load in enumerate(LOADS):
-            if load[0] == 1:
-                cast(i)
-        for h in range(2):
-            spread(h)
-        fetch(0)
+        for t in range(3):
+            for c in range(CHUNKS):
+                gather(c * CHUNK < VECTOR_SHARE[t], picked[c][:, t, :], planes[t], c * CHUNK, (c + 1) * CHUNK)
+            if t == 1:
+                for c in range(1, CHUNKS):
+                    merge(True, c, 0, 2)
+        merge(True, 0, 0, 3)
 
         x_codes = [keep.tile([P, CHUNK], U32, name=f"x_codes{c}", align_bytes=64) for c in range(CHUNKS)]
         x_scales = [keep.tile([P, CHUNK], U8, name=f"x_scales{c}", align_bytes=64) for c in range(CHUNKS)]
         acc = [psum.tile([P, CHUNK], F32, name=f"acc{c}") for c in range(CHUNKS)]
         result = [keep.tile([P, CHUNK], F32, name=f"result{c}") for c in range(CHUNKS)]
 
-        for c in range(CHUNKS):
-            gather(1, c)
-            nc.scalar.copy(out=woven[c][:], in_=picked[c][:].rearrange("p u n -> p n u"))
-        fetch(1)
-        for c in range(CHUNKS):
+        def multiply(c):
             nc.vector.quantize_mx(
                 out=x_codes[c][:].bitcast(FP8X4),
                 scales=x_scales[c][:],
-                in_=woven[c][:].rearrange("p n u -> p (n u)").bitcast(BF16),
+                in_=woven[c][:].rearrange("p n t -> p (n t)"),
             )
             nc.tensor.matmul_mx(
                 out=acc[c][:],
@@ -127,10 +116,26 @@ def tile_picked_tokscale_none_l_kernel(tc, xT, tscale, cscale, w1_words, w1_scal
                 start=True,
                 stop=True,
             )
-        for c in range(CHUNKS):
+
+        def finish(c):
             cols = slice(c * CHUNK, (c + 1) * CHUNK)
             factor = t_picked[c // 2][:, (c % 2) * CHUNK : (c % 2 + 1) * CHUNK]
             nc.vector.scalar_tensor_tensor(
                 out=result[c][:], in0=acc[c][:], scalar=c_col[:, 0:1], in1=factor, op0=MULT, op1=MULT
             )
             nc.sync.dma_start(out=out[:, cols], in_=result[c][:])
+
+        gather(True, woven[0][:, :, 3], planes[3], 0, CHUNK)
+        for c in range(1, CHUNKS):
+            gather(False, picked[c][:, 3, :], planes[3], c * CHUNK, (c + 1) * CHUNK)
+        merge(False, 3, 2, 4)
+        merge(True, 1, 2, 4)
+        multiply(0)
+        merge(True, 2, 2, 4)
+        multiply(1)
+        finish(0)
+        multiply(2)
+        finish(1)
+        multiply(3)
+        finish(2)
+        finish(3)

@@ -81,12 +81,12 @@ def tile_picked_tokscale_none_l_kernel(tc, xT, tscale, cscale, w1_words, w1_scal
         picked = [keep.tile([P, 4, CHUNK], BF16, name=f"picked{c}") for c in range(CHUNKS)]
         woven = [keep.tile([P, CHUNK, 4], BF16, name=f"woven{c}", align_bytes=64) for c in range(CHUNKS)]
 
-        def merge(on_vector, c, lo, hi):
-            src = picked[c][:, lo:hi, :].rearrange("p t n -> p n t")
+        def merge(on_vector, c, lo, hi, first=0, last=CHUNK):
+            src = picked[c][:, lo:hi, first:last].rearrange("p t n -> p n t")
             if on_vector:
-                nc.vector.tensor_copy(out=woven[c][:, :, lo:hi], in_=src)
+                nc.vector.tensor_copy(out=woven[c][:, first:last, lo:hi], in_=src)
             else:
-                nc.scalar.copy(out=woven[c][:, :, lo:hi], in_=src)
+                nc.scalar.copy(out=woven[c][:, first:last, lo:hi], in_=src)
 
         for t in range(3):
             for c in range(CHUNKS):
@@ -128,14 +128,13 @@ def tile_picked_tokscale_none_l_kernel(tc, xT, tscale, cscale, w1_words, w1_scal
         gather(True, woven[0][:, :, 3], planes[3], 0, CHUNK)
         for c in range(1, CHUNKS):
             gather(False, picked[c][:, 3, :], planes[3], c * CHUNK, (c + 1) * CHUNK)
-        merge(False, 3, 2, 4)
+        merge(False, 3, 2, 4, CHUNK // 2, CHUNK)
         merge(True, 1, 2, 4)
         multiply(0)
         merge(True, 2, 2, 4)
         multiply(1)
-        finish(0)
+        merge(True, 3, 2, 4, 0, CHUNK // 2)
         multiply(2)
-        finish(1)
         multiply(3)
-        finish(2)
-        finish(3)
+        for c in range(CHUNKS):
+            finish(c)

@@ -43,10 +43,10 @@ def tile_picked_tokscale_none_l_kernel(tc, xT, tscale, cscale, w1_words, w1_scal
         w_scales = keep.tile([P, N], U8, name="w_scales", align_bytes=64)
         c_col = keep.tile([P, 1], F32, name="c_col")
         nc.vector.memset(w_scales[:].bitcast(I32), 0)
+        nc.sync.dma_start(out=c_col[:], in_=cscale)
         nc.sync.dma_start(out=w_codes[:].bitcast(I32), in_=w1_words[0].rearrange("p n r -> p (n r)").bitcast(I32))
         for q in range(4):
             nc.sync.dma_start(out=w_scales[32 * q : 32 * q + 4, :].bitcast(I32), in_=w1_scales[0][4 * q : 4 * q + 4, :].bitcast(I32))
-        nc.sync.dma_start(out=c_col[:], in_=cscale)
 
         def entries(lo, hi):
             return offsets[:, lo // 16 : hi // 16]
@@ -96,45 +96,51 @@ def tile_picked_tokscale_none_l_kernel(tc, xT, tscale, cscale, w1_words, w1_scal
                     merge(True, c, 0, 2)
         merge(True, 0, 0, 3)
 
-        x_codes = [keep.tile([P, CHUNK], U32, name=f"x_codes{c}", align_bytes=64) for c in range(CHUNKS)]
-        x_scales = [keep.tile([P, CHUNK], U8, name=f"x_scales{c}", align_bytes=64) for c in range(CHUNKS)]
-        acc = [psum.tile([P, CHUNK], F32, name=f"acc{c}") for c in range(CHUNKS)]
-        result = [keep.tile([P, CHUNK], F32, name=f"result{c}") for c in range(CHUNKS)]
+        pieces = [(0, 0, CHUNK, 0, 0), (1, 0, CHUNK, 1, 0), (2, 0, CHUNK, 2, 0), (3, 0, CHUNK // 2, 2, CHUNK), (3, CHUNK // 2, CHUNK, 3, 0)]
+        cuts = [0, CHUNK, 2 * CHUNK, S - CHUNK // 2, S]
+        x_codes = [keep.tile([P, hi - lo], U32, name=f"x_codes{i}", align_bytes=64) for i, (c, lo, hi, b, at) in enumerate(pieces[:-1])]
+        x_codes.append(x_codes[0][:, 0 : CHUNK // 2])
+        x_scales = [keep.tile([P, hi - lo], U8, name=f"x_scales{i}", align_bytes=64) for i, (c, lo, hi, b, at) in enumerate(pieces)]
+        acc = [psum.tile([P, cuts[b + 1] - cuts[b]], F32, name=f"acc{b}") for b in range(4)]
+        result = [keep.tile([P, cuts[b + 1] - cuts[b]], F32, name=f"result{b}") for b in range(4)]
 
-        def multiply(c):
+        def multiply(i):
+            c, lo, hi, b, at = pieces[i]
             nc.vector.quantize_mx(
-                out=x_codes[c][:].bitcast(FP8X4),
-                scales=x_scales[c][:],
-                in_=woven[c][:].rearrange("p n t -> p (n t)"),
+                out=x_codes[i][:, 0 : hi - lo].bitcast(FP8X4),
+                scales=x_scales[i][:],
+                in_=woven[c][:, lo:hi, :].rearrange("p n t -> p (n t)"),
             )
             nc.tensor.matmul_mx(
-                out=acc[c][:],
+                out=acc[b][:, at : at + hi - lo],
                 lhsT=w_codes[:].bitcast(FP8X4),
                 lhsT_scale=w_scales[:],
-                rhs=x_codes[c][:].bitcast(FP8X4),
-                rhs_scale=x_scales[c][:],
+                rhs=x_codes[i][:, 0 : hi - lo].bitcast(FP8X4),
+                rhs_scale=x_scales[i][:],
                 start=True,
                 stop=True,
             )
 
-        def finish(c):
-            cols = slice(c * CHUNK, (c + 1) * CHUNK)
-            factor = t_picked[c // 2][:, (c % 2) * CHUNK : (c % 2 + 1) * CHUNK]
+        def finish(b):
+            lo, hi = cuts[b], cuts[b + 1]
+            factor = t_picked[lo // 512][:, lo % 512 : lo % 512 + hi - lo]
             nc.vector.scalar_tensor_tensor(
-                out=result[c][:], in0=acc[c][:], scalar=c_col[:, 0:1], in1=factor, op0=MULT, op1=MULT
+                out=result[b][:], in0=acc[b][:], scalar=c_col[:, 0:1], in1=factor, op0=MULT, op1=MULT
             )
-            nc.sync.dma_start(out=out[:, cols], in_=result[c][:])
+            nc.sync.dma_start(out=out[:, lo:hi], in_=result[b][:])
 
         gather(True, woven[0][:, :, 3], planes[3], 0, CHUNK)
-        for c in range(1, CHUNKS):
-            gather(False, picked[c][:, 3, :], planes[3], c * CHUNK, (c + 1) * CHUNK)
-        merge(False, 3, 2, 4, CHUNK // 2, CHUNK)
+        for c, lo, hi, b, at in pieces[1:]:
+            gather(False, picked[c][:, 3, lo:hi], planes[3], c * CHUNK + lo, c * CHUNK + hi)
+            if c == CHUNKS - 1:
+                merge(False, c, 2, 4, lo, hi)
         merge(True, 1, 2, 4)
         multiply(0)
         merge(True, 2, 2, 4)
         multiply(1)
-        merge(True, 3, 2, 4, 0, CHUNK // 2)
         multiply(2)
         multiply(3)
-        for c in range(CHUNKS):
-            finish(c)
+        finish(0)
+        multiply(4)
+        for b in range(1, 4):
+            finish(b)

@@ -18,9 +18,9 @@ MULT = mybir.AluOpType.mult
 COPY = mybir.ActivationFunctionType.Copy
 
 P = 128
-CHUNK = 256
-CHUNKS = S // CHUNK
-VECTOR_SHARE = [512, 256, 512]
+HALF = S // 2
+OWN = 320
+LAST = 768
 
 
 def tile_picked_tokscale_none_l_kernel(tc, xT, tscale, cscale, w1_words, w1_scales, offs, out):
@@ -48,22 +48,20 @@ def tile_picked_tokscale_none_l_kernel(tc, xT, tscale, cscale, w1_words, w1_scal
         for q in range(4):
             nc.sync.dma_start(out=w_scales[32 * q : 32 * q + 4, :].bitcast(I32), in_=w1_scales[0][4 * q : 4 * q + 4, :].bitcast(I32))
 
-        def entries(lo, hi):
-            return offsets[:, lo // 16 : hi // 16]
-
         def gather(on_vector, dst, window, lo, hi):
+            looked_up = window[:].indirect(offsets[:, lo // 16 : hi // 16])
             if on_vector:
-                nc.vector.tensor_copy(out=dst, in_=window[:].indirect(entries(lo, hi)))
+                nc.vector.tensor_copy(out=dst, in_=looked_up)
             else:
-                nc.scalar.activation(dst, window[:].indirect(entries(lo, hi)), COPY)
+                nc.scalar.activation(dst, looked_up, COPY)
 
         identity = keep.tile([P, P], F32, name="identity")
         make_identity(nc, identity[:])
-        t_row = [keep.tile([P, 512], F32, name=f"t_row{h}") for h in range(2)]
+        t_row = [keep.tile([P, HALF], F32, name=f"t_row{h}") for h in range(2)]
         t_col = [keep.tile([P, 4], F32, name=f"t_col{h}") for h in range(2)]
-        t_picked = [keep.tile([P, 512], F32, name=f"t_picked{h}") for h in range(2)]
+        t_picked = [keep.tile([P, HALF], F32, name=f"t_picked{h}") for h in range(2)]
         for h in range(2):
-            gather(h == 0, t_row[h][:], t_window, 512 * h, 512 * (h + 1))
+            gather(h == 0, t_row[h][:], t_window, HALF * h, HALF * (h + 1))
         for h in range(2):
             turned = psum.tile([P, 4, P], F32, name=f"turned{h}")
             for i in range(4):
@@ -78,41 +76,50 @@ def tile_picked_tokscale_none_l_kernel(tc, xT, tscale, cscale, w1_words, w1_scal
             else:
                 nc.scalar.copy(out=t_picked[h][:], in_=wide[:].rearrange("f i p -> f (i p)"))
 
-        picked = [keep.tile([P, 4, CHUNK], BF16, name=f"picked{c}") for c in range(CHUNKS)]
-        woven = [keep.tile([P, CHUNK, 4], BF16, name=f"woven{c}", align_bytes=64) for c in range(CHUNKS)]
+        picked = keep.tile([P, 4, S], BF16, name="picked")
+        woven = keep.tile([P, S, 4], BF16, name="woven", align_bytes=64)
 
-        def merge(on_vector, c, lo, hi, first=0, last=CHUNK):
-            src = picked[c][:, lo:hi, first:last].rearrange("p t n -> p n t")
+        def pick(on_vector, t, lo, hi):
+            gather(on_vector, picked[:, t, lo:hi], planes[t], lo, hi)
+
+        def merge(on_vector, first, last, lo, hi):
+            src = picked[:, first:last, lo:hi].rearrange("p t n -> p n t")
             if on_vector:
-                nc.vector.tensor_copy(out=woven[c][:, first:last, lo:hi], in_=src)
+                nc.vector.tensor_copy(out=woven[:, lo:hi, first:last], in_=src)
             else:
-                nc.scalar.copy(out=woven[c][:, first:last, lo:hi], in_=src)
+                nc.scalar.copy(out=woven[:, lo:hi, first:last], in_=src)
 
-        for t in range(3):
-            for c in range(CHUNKS):
-                gather(c * CHUNK < VECTOR_SHARE[t], picked[c][:, t, :], planes[t], c * CHUNK, (c + 1) * CHUNK)
-            if t == 1:
-                for c in range(1, CHUNKS):
-                    merge(True, c, 0, 2)
-        merge(True, 0, 0, 3)
+        pick(True, 0, 0, 576)
+        pick(False, 0, 576, S)
+        pick(True, 1, OWN, 512)
+        pick(True, 1, 512, 704)
+        pick(False, 1, 704, S)
+        pick(False, 1, 0, OWN)
+        merge(True, 0, 2, OWN, 512)
+        merge(True, 0, 2, 704, S)
+        merge(True, 0, 2, 512, 704)
+        pick(True, 2, 0, OWN)
+        pick(True, 2, OWN, 448)
+        pick(False, 2, 448, S)
+        merge(True, 0, 3, 0, OWN)
 
-        pieces = [(0, 0, CHUNK, 0, 0), (1, 0, CHUNK, 1, 0), (2, 0, CHUNK, 2, 0), (3, 0, CHUNK // 2, 2, CHUNK), (3, CHUNK // 2, CHUNK, 3, 0)]
-        cuts = [0, CHUNK, 2 * CHUNK, S - CHUNK // 2, S]
-        x_codes = [keep.tile([P, hi - lo], U32, name=f"x_codes{i}", align_bytes=64) for i, (c, lo, hi, b, at) in enumerate(pieces[:-1])]
-        x_codes.append(x_codes[0][:, 0 : CHUNK // 2])
-        x_scales = [keep.tile([P, hi - lo], U8, name=f"x_scales{i}", align_bytes=64) for i, (c, lo, hi, b, at) in enumerate(pieces)]
+        pieces = [(0, 256, 0), (256, 512, 1), (512, 768, 2), (768, 896, 2), (896, S, 3)]
+        cuts = [0, 256, 512, 896, S]
+        x_codes = [keep.tile([P, hi - lo], U32, name=f"x_codes{i}", align_bytes=64) for i, (lo, hi, b) in enumerate(pieces[:-1])]
+        x_codes.append(x_codes[0][:, 0:128])
+        x_scales = [keep.tile([P, hi - lo], U8, name=f"x_scales{i}", align_bytes=64) for i, (lo, hi, b) in enumerate(pieces)]
         acc = [psum.tile([P, cuts[b + 1] - cuts[b]], F32, name=f"acc{b}") for b in range(4)]
         result = [keep.tile([P, cuts[b + 1] - cuts[b]], F32, name=f"result{b}") for b in range(4)]
 
         def multiply(i):
-            c, lo, hi, b, at = pieces[i]
+            lo, hi, b = pieces[i]
             nc.vector.quantize_mx(
                 out=x_codes[i][:, 0 : hi - lo].bitcast(FP8X4),
                 scales=x_scales[i][:],
-                in_=woven[c][:, lo:hi, :].rearrange("p n t -> p (n t)"),
+                in_=woven[:, lo:hi, :].rearrange("p n t -> p (n t)"),
             )
             nc.tensor.matmul_mx(
-                out=acc[b][:, at : at + hi - lo],
+                out=acc[b][:, lo - cuts[b] : hi - cuts[b]],
                 lhsT=w_codes[:].bitcast(FP8X4),
                 lhsT_scale=w_scales[:],
                 rhs=x_codes[i][:, 0 : hi - lo].bitcast(FP8X4),
@@ -123,24 +130,26 @@ def tile_picked_tokscale_none_l_kernel(tc, xT, tscale, cscale, w1_words, w1_scal
 
         def finish(b):
             lo, hi = cuts[b], cuts[b + 1]
-            factor = t_picked[lo // 512][:, lo % 512 : lo % 512 + hi - lo]
+            factor = t_picked[lo // HALF][:, lo % HALF : lo % HALF + hi - lo]
             nc.vector.scalar_tensor_tensor(
                 out=result[b][:], in0=acc[b][:], scalar=c_col[:, 0:1], in1=factor, op0=MULT, op1=MULT
             )
             nc.sync.dma_start(out=out[:, lo:hi], in_=result[b][:])
 
-        gather(True, woven[0][:, :, 3], planes[3], 0, CHUNK)
-        for c, lo, hi, b, at in pieces[1:]:
-            gather(False, picked[c][:, 3, lo:hi], planes[3], c * CHUNK + lo, c * CHUNK + hi)
-            if c == CHUNKS - 1:
-                merge(False, c, 2, 4, lo, hi)
-        merge(True, 1, 2, 4)
+        gather(True, woven[:, 0:OWN, 3], planes[3], 0, OWN)
+        pick(False, 3, OWN, 576)
+        pick(False, 3, 576, LAST)
+        pick(False, 3, LAST, 896)
+        pick(False, 3, 896, S)
+        merge(False, 2, 4, LAST, 896)
+        merge(False, 2, 4, 896, S)
+        merge(True, 2, 4, OWN, 576)
         multiply(0)
-        merge(True, 2, 2, 4)
+        merge(True, 2, 4, 576, LAST)
         multiply(1)
         multiply(2)
-        multiply(3)
         finish(0)
+        multiply(3)
         multiply(4)
         for b in range(1, 4):
             finish(b)

@@ -103,10 +103,10 @@ def tile_picked_tokscale_none_l_kernel(tc, xT, tscale, cscale, w1_words, w1_scal
         pick(False, 2, 448, S)
         merge(True, 0, 3, 0, OWN)
 
-        pieces = [(0, 256, 0), (256, 512, 1), (512, 768, 2), (768, 896, 2), (896, S, 3)]
-        cuts = [0, 256, 512, 896, S]
-        x_codes = [keep.tile([P, hi - lo], U32, name=f"x_codes{i}", align_bytes=64) for i, (lo, hi, b) in enumerate(pieces[:-1])]
-        x_codes.append(x_codes[0][:, 0:128])
+        pieces = [(0, 256, 0), (256, 512, 1), (512, 768, 2), (768, 896, 3), (896, S, 3)]
+        cuts = [0, 256, 512, 768, S]
+        x_codes = [keep.tile([P, hi - lo], U32, name=f"x_codes{i}", align_bytes=64) for i, (lo, hi, b) in enumerate(pieces[:3])]
+        x_codes[3:] = [x_codes[0][:, 0:128], x_codes[0][:, 128:256]]
         x_scales = [keep.tile([P, hi - lo], U8, name=f"x_scales{i}", align_bytes=64) for i, (lo, hi, b) in enumerate(pieces)]
         acc = [psum.tile([P, cuts[b + 1] - cuts[b]], F32, name=f"acc{b}") for b in range(4)]
         result = [keep.tile([P, cuts[b + 1] - cuts[b]], F32, name=f"result{b}") for b in range(4)]

@@ -19,7 +19,7 @@ COPY = mybir.ActivationFunctionType.Copy
 
 P = 128
 HALF = S // 2
-OWN = 320
+OWN = 256
 LAST = 768
 
 
@@ -76,7 +76,7 @@ def tile_picked_tokscale_none_l_kernel(tc, xT, tscale, cscale, w1_words, w1_scal
             else:
                 nc.scalar.copy(out=t_picked[h][:], in_=wide[:].rearrange("f i p -> f (i p)"))
 
-        picked = keep.tile([P, 4, S], BF16, name="picked")
+        picked = keep.tile([P, 4, S], F32, name="picked")
         woven = keep.tile([P, S, 4], BF16, name="woven", align_bytes=64)
 
         def pick(on_vector, t, lo, hi):
@@ -92,12 +92,12 @@ def tile_picked_tokscale_none_l_kernel(tc, xT, tscale, cscale, w1_words, w1_scal
         pick(True, 0, 0, 576)
         pick(False, 0, 576, S)
         pick(True, 1, OWN, 512)
-        pick(True, 1, 512, 704)
-        pick(False, 1, 704, S)
+        pick(True, 1, 512, 640)
+        pick(False, 1, 640, S)
         pick(False, 1, 0, OWN)
         merge(True, 0, 2, OWN, 512)
-        merge(True, 0, 2, 704, S)
-        merge(True, 0, 2, 512, 704)
+        merge(True, 0, 2, 640, S)
+        merge(True, 0, 2, 512, 640)
         pick(True, 2, 0, OWN)
         pick(True, 2, OWN, 448)
         pick(False, 2, 448, S)
@@ -137,15 +137,15 @@ def tile_picked_tokscale_none_l_kernel(tc, xT, tscale, cscale, w1_words, w1_scal
             nc.sync.dma_start(out=out[:, lo:hi], in_=result[b][:])
 
         gather(True, woven[:, 0:OWN, 3], planes[3], 0, OWN)
-        pick(False, 3, OWN, 576)
-        pick(False, 3, 576, LAST)
+        pick(False, 3, OWN, 512)
+        pick(False, 3, 512, LAST)
         pick(False, 3, LAST, 896)
         pick(False, 3, 896, S)
         merge(False, 2, 4, LAST, 896)
         merge(False, 2, 4, 896, S)
-        merge(True, 2, 4, OWN, 576)
+        merge(True, 2, 4, OWN, 512)
         multiply(0)
-        merge(True, 2, 4, 576, LAST)
+        merge(True, 2, 4, 512, LAST)
         multiply(1)
         multiply(2)
         finish(0)

@@ -99,8 +99,8 @@ def tile_picked_tokscale_none_l_kernel(tc, xT, tscale, cscale, w1_words, w1_scal
         merge(True, 0, 2, 640, S)
         merge(True, 0, 2, 512, 640)
         pick(True, 2, 0, OWN)
-        pick(True, 2, OWN, 448)
-        pick(False, 2, 448, S)
+        pick(True, 2, OWN, 384)
+        pick(False, 2, 384, S)
         merge(True, 0, 3, 0, OWN)
 
         pieces = [(0, 256, 0), (256, 512, 1), (512, 768, 2), (768, 896, 3), (896, S, 3)]

@@ -34,7 +34,7 @@ def tile_picked_tokscale_none_l_kernel(tc, xT, tscale, cscale, w1_words, w1_scal
         planes = [keep.tile([P, T], F32, name=f"plane{t}") for t in range(4)]
         t_window = keep.tile([P, T], F32, name="t_window")
         nc.vector.memset(t_window[0 : P - 1, :], 0.0)
-        nc.sync.dma_start(out=t_window[P - 1 : P, :], in_=tscale[0:1, :])
+        nc.scalar.dma_start(out=t_window[P - 1 : P, :], in_=tscale[0:1, :])
         nc.sync.dma_start(offsets[:], offs)
         for t in range(4):
             nc.sync.dma_start(out=planes[t][:], in_=x_rows[t])

@@ -19,6 +19,7 @@ COPY = mybir.ActivationFunctionType.Copy
 
 P = 128
 HALF = S // 2
+SHARED = 128
 OWN = 256
 LAST = 768
 
@@ -33,7 +34,9 @@ def tile_picked_tokscale_none_l_kernel(tc, xT, tscale, cscale, w1_words, w1_scal
         x_rows = xT.rearrange("(p t) c -> t p c", t=4)
         planes = [keep.tile([P, T], F32, name=f"plane{t}") for t in range(4)]
         t_window = keep.tile([P, T], F32, name="t_window")
-        nc.vector.memset(t_window[0 : P - 1, :], 0.0)
+        nc.vector.memset(t_window[0 : P - 1, 0:SHARED], 0.0)
+        nc.vector.memset(t_window[0 : P - 1, SHARED : T - SHARED].bitcast(I32), 0)
+        nc.scalar.copy(out=t_window[0 : P - 1, T - SHARED : T], in_=t_window[0 : P - 1, 0:SHARED])
         nc.scalar.dma_start(out=t_window[P - 1 : P, :], in_=tscale[0:1, :])
         nc.sync.dma_start(offsets[:], offs)
         for t in range(4):

@@ -143,12 +143,13 @@ def tile_picked_tokscale_none_l_kernel(tc, xT, tscale, cscale, w1_words, w1_scal
         pick(False, 3, OWN, 512)
         pick(False, 3, 512, LAST)
         pick(False, 3, LAST, 896)
+        merge(False, 2, 4, 704, LAST)
         pick(False, 3, 896, S)
         merge(False, 2, 4, LAST, 896)
         merge(False, 2, 4, 896, S)
         merge(True, 2, 4, OWN, 512)
         multiply(0)
-        merge(True, 2, 4, 512, LAST)
+        merge(True, 2, 4, 512, 704)
         multiply(1)
         multiply(2)
         finish(0)

from contextlib import ExitStack

import concourse.mybir as mybir
from concourse.masks import make_identity

K, T, S, N = 512, 2048, 1024, 128
FLOPS = 2 * K * N * S
BYTES = 4 * K * T + 4 * T + 4 * N + K * N + 16 * N + 2 * 128 * (S // 16) + 4 * N * S

F32 = mybir.dt.float32
BF16 = mybir.dt.bfloat16
U32 = mybir.dt.uint32
I32 = mybir.dt.int32
U16 = mybir.dt.uint16
U8 = mybir.dt.uint8
FP8X4 = mybir.dt.float8_e4m3fn_x4
MULT = mybir.AluOpType.mult
COPY = mybir.ActivationFunctionType.Copy

P = 128
HALF = S // 2
SHARED = 128
OWN = 256
LAST = 768


def tile_picked_tokscale_none_l_kernel(tc, xT, tscale, cscale, w1_words, w1_scales, offs, out):
    nc = tc.nc
    with ExitStack() as ctx:
        keep = ctx.enter_context(tc.tile_pool(name="keep", bufs=1))
        psum = ctx.enter_context(tc.psum_pool(name="psum", bufs=1))

        offsets = keep.tile([P, S // 16], U16, name="offsets")
        x_rows = xT.rearrange("(p t) c -> t p c", t=4)
        planes = [keep.tile([P, T], F32, name=f"plane{t}") for t in range(4)]
        t_window = keep.tile([P, T], F32, name="t_window")
        nc.vector.memset(t_window[0 : P - 1, 0:SHARED], 0.0)
        nc.vector.memset(t_window[0 : P - 1, SHARED : T - SHARED].bitcast(I32), 0)
        nc.scalar.copy(out=t_window[0 : P - 1, T - SHARED : T], in_=t_window[0 : P - 1, 0:SHARED])
        nc.scalar.dma_start(out=t_window[P - 1 : P, :], in_=tscale[0:1, :])
        nc.sync.dma_start(offsets[:], offs)
        for t in range(4):
            nc.sync.dma_start(out=planes[t][:], in_=x_rows[t])

        w_codes = keep.tile([P, N], U32, name="w_codes", align_bytes=64)
        w_scales = keep.tile([P, N], U8, name="w_scales", align_bytes=64)
        c_col = keep.tile([P, 1], F32, name="c_col")
        nc.vector.memset(w_scales[:].bitcast(I32), 0)
        nc.sync.dma_start(out=c_col[:], in_=cscale)
        nc.sync.dma_start(out=w_codes[:].bitcast(I32), in_=w1_words[0].rearrange("p n r -> p (n r)").bitcast(I32))
        for q in range(4):
            nc.sync.dma_start(out=w_scales[32 * q : 32 * q + 4, :].bitcast(I32), in_=w1_scales[0][4 * q : 4 * q + 4, :].bitcast(I32))

        def gather(on_vector, dst, window, lo, hi):
            looked_up = window[:].indirect(offsets[:, lo // 16 : hi // 16])
            if on_vector:
                nc.vector.tensor_copy(out=dst, in_=looked_up)
            else:
                nc.scalar.activation(dst, looked_up, COPY)

        identity = keep.tile([P, P], F32, name="identity")
        make_identity(nc, identity[:])
        t_row = [keep.tile([P, HALF], F32, name=f"t_row{h}") for h in range(2)]
        t_col = [keep.tile([P, 4], F32, name=f"t_col{h}") for h in range(2)]
        t_picked = [keep.tile([P, HALF], F32, name=f"t_picked{h}") for h in range(2)]
        for h in range(2):
            gather(h == 0, t_row[h][:], t_window, HALF * h, HALF * (h + 1))
        for h in range(2):
            turned = psum.tile([P, 4, P], F32, name=f"turned{h}")
            for i in range(4):
                nc.tensor.transpose(turned[:, i, :], t_row[h][:, i * P : (i + 1) * P], identity[:])
            nc.scalar.copy(out=t_col[h][:], in_=turned[:, :, P - 1])
        for h in range(2):
            wide = psum.tile([P, 4, P], F32, name=f"wide{h}")
            for i in range(4):
                nc.tensor.transpose(wide[:, i, :], t_col[h][:, i : i + 1].to_broadcast([P, P]), identity[:])
            if h == 0:
                nc.vector.tensor_copy(out=t_picked[h][:], in_=wide[:].rearrange("f i p -> f (i p)"))
            else:
                nc.scalar.copy(out=t_picked[h][:], in_=wide[:].rearrange("f i p -> f (i p)"))

        picked = keep.tile([P, 4, S], F32, name="picked")
        woven = keep.tile([P, S, 4], BF16, name="woven", align_bytes=64)

        def pick(on_vector, t, lo, hi):
            gather(on_vector, picked[:, t, lo:hi], planes[t], lo, hi)

        def merge(on_vector, first, last, lo, hi):
            src = picked[:, first:last, lo:hi].rearrange("p t n -> p n t")
            if on_vector:
                nc.vector.tensor_copy(out=woven[:, lo:hi, first:last], in_=src)
            else:
                nc.scalar.copy(out=woven[:, lo:hi, first:last], in_=src)

        pick(True, 0, 0, 576)
        pick(False, 0, 576, S)
        pick(True, 1, OWN, 512)
        pick(True, 1, 512, 640)
        pick(False, 1, 640, S)
        pick(False, 1, 0, OWN)
        merge(True, 0, 2, OWN, 512)
        merge(True, 0, 2, 640, S)
        merge(True, 0, 2, 512, 640)
        pick(True, 2, 0, OWN)
        pick(True, 2, OWN, 384)
        pick(False, 2, 384, S)
        merge(True, 0, 3, 0, OWN)

        pieces = [(0, 256, 0), (256, 512, 1), (512, 768, 2), (768, 896, 3), (896, S, 3)]
        cuts = [0, 256, 512, 768, S]
        x_codes = [keep.tile([P, hi - lo], U32, name=f"x_codes{i}", align_bytes=64) for i, (lo, hi, b) in enumerate(pieces[:3])]
        x_codes[3:] = [x_codes[0][:, 0:128], x_codes[0][:, 128:256]]
        x_scales = [keep.tile([P, hi - lo], U8, name=f"x_scales{i}", align_bytes=64) for i, (lo, hi, b) in enumerate(pieces)]
        acc = [psum.tile([P, cuts[b + 1] - cuts[b]], F32, name=f"acc{b}") for b in range(4)]
        result = [keep.tile([P, cuts[b + 1] - cuts[b]], F32, name=f"result{b}") for b in range(4)]

        def multiply(i):
            lo, hi, b = pieces[i]
            nc.vector.quantize_mx(
                out=x_codes[i][:, 0 : hi - lo].bitcast(FP8X4),
                scales=x_scales[i][:],
                in_=woven[:, lo:hi, :].rearrange("p n t -> p (n t)"),
            )
            nc.tensor.matmul_mx(
                out=acc[b][:, lo - cuts[b] : hi - cuts[b]],
                lhsT=w_codes[:].bitcast(FP8X4),
                lhsT_scale=w_scales[:],
                rhs=x_codes[i][:, 0 : hi - lo].bitcast(FP8X4),
                rhs_scale=x_scales[i][:],
                start=True,
                stop=True,
            )

        def finish(b):
            lo, hi = cuts[b], cuts[b + 1]
            factor = t_picked[lo // HALF][:, lo % HALF : lo % HALF + hi - lo]
            nc.vector.scalar_tensor_tensor(
                out=result[b][:], in0=acc[b][:], scalar=c_col[:, 0:1], in1=factor, op0=MULT, op1=MULT
            )
            nc.sync.dma_start(out=out[:, lo:hi], in_=result[b][:])

        gather(True, woven[:, 0:OWN, 3], planes[3], 0, OWN)
        pick(False, 3, OWN, 512)
        pick(False, 3, 512, LAST)
        pick(False, 3, LAST, 896)
        merge(False, 2, 4, 704, LAST)
        pick(False, 3, 896, S)
        merge(False, 2, 4, LAST, 896)
        merge(False, 2, 4, 896, S)
        merge(True, 2, 4, OWN, 512)
        multiply(0)
        merge(True, 2, 4, 512, 704)
        multiply(1)
        multiply(2)
        finish(0)
        multiply(3)
        multiply(4)
        for b in range(1, 4):
            finish(b)
